import numpy as np
import ml_dtypes


def mxq(x, axis, fmt="e4m3"):
    dtype, down = {"e4m3": (ml_dtypes.float8_e4m3fn, 7), "e5m2": (ml_dtypes.float8_e5m2, 14)}[fmt]
    v = np.moveaxis(np.asarray(x, np.float32).astype(ml_dtypes.bfloat16).astype(np.float64), axis, -1)
    blocks = v.reshape(v.shape[:-1] + (-1, 32))
    amax = np.abs(blocks).max(-1, keepdims=True)
    byte = np.maximum(np.where(amax > 0, np.frexp(amax)[1] - 1 + 127, 0) - down, 1)
    scale = np.exp2(byte - 127.0)
    codes = (blocks / scale).astype(np.float32).astype(dtype).astype(np.float64)
    return np.moveaxis((codes * scale).reshape(v.shape), -1, axis)


WIDE = False


def mx_kscale(k):
    if not WIDE:
        return np.ones(k)
    levels = np.array([10, -10, 5, -5, 0])
    if k % 512:
        return np.exp2(np.random.permutation(np.resize(levels, k // 32))).repeat(32)
    a = np.empty((k // 512, 16))
    for p in range(k // 512):
        a[p, :8] = np.random.permutation(np.resize(levels, 8))
        for g in range(8):
            far = levels[np.abs(levels - a[p, g]) >= 10]
            a[p, g + 8] = far[np.random.randint(len(far))]
    return np.exp2(a.ravel()).repeat(32)


def f64(x):
    return np.asarray(x).astype(np.float64)


def striped(idx):
    return np.tile(idx.reshape(-1, 16).T, (8, 1)).astype(np.uint16)


def unstriped(offs):
    return offs[:16].T.reshape(-1).astype(np.int64)


E2M1 = np.array([0.0, 0.5, 1.0, 1.5, 2.0, 3.0, 4.0, 6.0, -0.0, -0.5, -1.0, -1.5, -2.0, -3.0, -4.0, -6.0])


def pack_weight(w, fmt):
    k, n = w.shape
    w = f64(np.asarray(w, np.float32).astype(ml_dtypes.bfloat16)).reshape(k // 32, 32, n)
    amax = np.abs(w).max(1)
    if fmt == "e4m3":
        byte = np.frexp(amax)[1] - 1 + 127 - 7
    else:
        mant, ex = np.frexp(amax / 6.0)
        byte = np.where(mant > 0.5, ex, ex - 1) + 127
    byte = np.clip(np.where(amax > 0, byte, 1), 1, 254)
    scaled = (w * np.exp2(127.0 - byte)[:, None, :]).reshape(k, n).astype(np.float32)
    by_word = np.ascontiguousarray(scaled.reshape(k // 512, 128, 4, n).transpose(0, 1, 3, 2))
    if fmt == "e4m3":
        words = by_word.astype(ml_dtypes.float8_e4m3fn).view(np.uint8)
    else:
        c = by_word.astype(ml_dtypes.float4_e2m1fn).view(np.uint8) & 0xF
        words = (c[..., 0::2] | (c[..., 1::2] << 4)).reshape(k // 512, 128, 2 * n)
    return np.ascontiguousarray(words), np.ascontiguousarray(byte.astype(np.uint8).reshape(k // 512, 16, n))


def unpack_weight(words, scales, fmt):
    g, _, n = scales.shape
    words = np.ascontiguousarray(words).reshape(g, 128, n, -1)
    if fmt == "e4m3":
        vals = words.view(ml_dtypes.float8_e4m3fn).astype(np.float64)
    else:
        nib = np.empty((g, 128, n, 4), np.uint8)
        nib[..., 0::2] = words & 0xF
        nib[..., 1::2] = words >> 4
        vals = E2M1[nib]
    vals = vals * np.repeat(np.exp2(scales.astype(np.float64) - 127.0), 8, axis=1)[..., None]
    return vals.transpose(0, 1, 3, 2).reshape(g * 512, n)


def gelu(v):
    return 0.5 * v * (1.0 + np.tanh(np.sqrt(2.0 / np.pi) * (v + 0.044715 * v**3)))


K, T, S, S2 = 1024, 2048, 512, 1024

def setup_inputs():
    n = np.random.standard_normal
    s = mx_kscale(K)[:, None]
    d = {}
    d["tab_words"], d["tab_scales"] = pack_weight(n((K, T)) * s, "e4m3")
    d["offs"] = striped(np.random.permutation(T)[:S])
    d["offs2"] = striped(np.random.permutation(T)[:S2])
    d["w"] = (n((K, K)) / s / s.T / K).astype(np.float32)
    d["wb_words"], d["wb_scales"] = pack_weight(n((K, K)) / s / K**0.5, "e2m1")
    d["gain"] = (np.exp(0.4 * n(K)) / s[:, 0] / K**0.5).astype(np.float32)
    d["w2"] = (n((K, S2)) * s).astype(np.float32)
    d["seat"] = np.exp(0.4 * n((S2, S))).astype(np.float32)
    return d

def reference(tab_words, tab_scales, offs, offs2, w, wb_words, wb_scales, gain, w2, seat):
    TW = unpack_weight(tab_words, tab_scales, "e4m3")
    v = TW[:, unstriped(offs)]
    v2 = TW[:, unstriped(offs2)]
    h = np.abs(mxq(f64(w), 0, "e4m3").T @ v)
    hq = mxq(h, 0, "e4m3")
    x = f64(gain)[:, None] * (unpack_weight(wb_words, wb_scales, "e2m1").T @ v)
    xq = mxq(x, 0, "e4m3")
    e = v2.T @ hq
    b = v2.T @ xq
    f = mxq(f64(w2), 0, "e4m3").T @ hq
    return (e - np.maximum(f, b)) * f64(seat)

@@ -1,0 +1,276 @@
+from contextlib import ExitStack
+
+import concourse.mybir as mybir
+
+K, T, S, S2 = 1024, 2048, 512, 1024
+FLOPS = 2 * K * K * S * 2 + 2 * K * S2 * S * 3
+
+F32 = mybir.dt.float32
+BF16 = mybir.dt.bfloat16
+I32 = mybir.dt.int32
+U32 = mybir.dt.uint32
+U16 = mybir.dt.uint16
+U8 = mybir.dt.uint8
+FP8X4 = mybir.dt.float8_e4m3fn_x4
+FP4X4 = mybir.dt.float4_e2m1fn_x4
+ALU = mybir.AluOpType
+ACT = mybir.ActivationFunctionType
+
+P = 128
+PACK = 4
+KP = P * PACK
+NPASS = K // KP
+JT = 128
+W2C = 256
+GC = 256
+
+
+def tile_list_table_companion_ease_kernel(
+    tc, tab_words, tab_scales, offs, offs2, w, wb_words, wb_scales, gain, w2, seat, out
+):
+    nc = tc.nc
+    with ExitStack() as ctx:
+        keep = ctx.enter_context(tc.tile_pool(name="keep", bufs=1))
+        ring = ctx.enter_context(tc.tile_pool(name="ring", bufs=3))
+        ring2 = ctx.enter_context(tc.tile_pool(name="ring2", bufs=2))
+        psum = ctx.enter_context(tc.psum_pool(name="psum", bufs=4))
+
+        def held(shape, dtype, name):
+            return keep.tile(shape, dtype, name=name, align_bytes=64)
+
+        o1 = keep.tile([P, S // 16], U16, name="o1")
+        o2 = keep.tile([P, S2 // 16], U16, name="o2")
+        sc_both = held([P, T], U8, "sc_both")
+        wbs_raw = held([P, NPASS * K], U8, "wbs_raw")
+        nc.vector.memset(sc_both[:].bitcast(I32), 0)
+        nc.gpsimd.memset(wbs_raw[:].bitcast(I32), 0)
+
+        tw = [held([P, T], U32, "tw%d" % a) for a in range(NPASS)]
+        wraw = {}
+        for a in range(NPASS):
+            for b in range(NPASS):
+                wraw[a, b] = held([P, PACK, KP], F32, "wraw%d%d" % (a, b))
+        wbw_raw = held([P, NPASS, 2 * K], U8, "wbw_raw")
+        g = held([P, NPASS, PACK], F32, "g")
+
+        def load_w(a, b):
+            nc.sync.dma_start(
+                out=wraw[a, b][:],
+                in_=w[a * KP : (a + 1) * KP, b * KP : (b + 1) * KP].rearrange("(p j) c -> p j c", j=PACK),
+            )
+
+        def load_tab(a):
+            nc.sync.dma_start(
+                out=tw[a][:].bitcast(I32),
+                in_=tab_words[a].rearrange("p t i -> p (t i)").bitcast(I32),
+            )
+
+        vs_hi = held([P, S], U8, "vs_hi")
+        nc.gpsimd.memset(vs_hi[:].bitcast(I32), 0)
+        ts32 = tab_scales.bitcast(I32)
+        ws32 = wb_scales.bitcast(I32)
+        nc.sync.dma_start(o1[:], offs)
+        nc.sync.dma_start(o2[:], offs2)
+        nc.sync.dma_start(out=g[:], in_=gain.rearrange("(b p t) -> p b t", b=NPASS, t=PACK))
+        for q in range(4):
+            nc.sync.dma_start(
+                out=sc_both[:].bitcast(I32)[32 * q : 32 * q + 8, :],
+                in_=ts32[:, 4 * q : 4 * q + 4, :],
+            )
+        load_w(0, 0)
+        load_tab(0)
+        load_w(1, 0)
+        load_tab(1)
+        for q in range(4):
+            nc.sync.dma_start(
+                out=wbs_raw[:].bitcast(I32)[32 * q : 32 * q + 4, :].rearrange("r (a c) -> r a c", a=NPASS),
+                in_=ws32[:, 4 * q : 4 * q + 4, :].rearrange("a r c -> r a c"),
+            )
+        nc.sync.dma_start(
+            out=wbw_raw[:].rearrange("p a c -> p (a c)").bitcast(I32).rearrange("p (a c) -> p a c", a=NPASS),
+            in_=wb_words.bitcast(I32).rearrange("a p c -> p a c"),
+        )
+        load_w(0, 1)
+        load_w(1, 1)
+
+        w2raw = {}
+        seat_t = {}
+        for c in range(S2 // W2C):
+            for b in range(NPASS):
+                w2raw[c, b] = held([P, PACK, W2C], F32, "w2raw%d%d" % (c, b))
+                nc.sync.dma_start(
+                    out=w2raw[c, b][:],
+                    in_=w2[b * KP : (b + 1) * KP, c * W2C : (c + 1) * W2C].rearrange("(p j) c -> p j c", j=PACK),
+                )
+            if c > 0:
+                seat_t[c - 1] = held([P, 2, S], F32, "seat%d" % (c - 1))
+                nc.sync.dma_start(
+                    out=seat_t[c - 1][:],
+                    in_=seat[(c - 1) * W2C : c * W2C, :].rearrange("(u p) j -> p u j", p=P),
+                )
+        c = S2 // W2C - 1
+        seat_t[c] = held([P, 2, S], F32, "seat%d" % c)
+        nc.sync.dma_start(
+            out=seat_t[c][:], in_=seat[c * W2C : (c + 1) * W2C, :].rearrange("(u p) j -> p u j", p=P)
+        )
+
+        vs = held([P, S], U8, "vs")
+        vw = [held([P, S], U32, "vw%d" % a) for a in range(NPASS)]
+        nc.vector.tensor_copy(vs[:], sc_both[:].indirect(o1[:]))
+        for q in range(4):
+            nc.gpsimd.dma_start(
+                out=vs_hi[:].bitcast(I32)[32 * q : 32 * q + 4, :],
+                in_=vs[:].bitcast(I32)[32 * q + 4 : 32 * q + 8, :],
+            )
+        v2s = [held([P, GC], U8, "v2s%d" % c) for c in range(S2 // GC)]
+        v2w = {}
+
+        def gather2_scales(c):
+            nc.vector.tensor_copy(v2s[c][:], sc_both[:].indirect(o2[:, c * GC // 16 : (c + 1) * GC // 16]))
+
+        def gather2_words(c):
+            for a in range(NPASS):
+                v2w[c, a] = ring2.tile([P, GC], U32, name="v2w%d" % a, align_bytes=64)
+                nc.vector.tensor_copy(v2w[c, a][:], tw[a][:].indirect(o2[:, c * GC // 16 : (c + 1) * GC // 16]))
+
+        for c in range(S2 // GC):
+            gather2_scales(c)
+        nc.vector.tensor_copy(vw[0][:], tw[0][:].indirect(o1[:]))
+
+        wbs = held([P, NPASS * K], U8, "wbs")
+        wbw = held([P, NPASS * 2 * K], U8, "wbw")
+        nc.vector.tensor_copy(
+            out=wbs[:].rearrange("p (u t m) -> p u m t", t=PACK, m=P),
+            in_=wbs_raw[:].rearrange("p (u m t) -> p u m t", t=PACK, m=P),
+        )
+        nc.vector.tensor_copy(vw[1][:], tw[1][:].indirect(o1[:]))
+        nc.vector.tensor_copy(
+            out=wbw[:].bitcast(U16).rearrange("p (u t m) -> p u m t", t=PACK, m=P),
+            in_=wbw_raw[:].rearrange("p a c -> p (a c)").bitcast(U16).rearrange("p (u m t) -> p u m t", t=PACK, m=P),
+        )
+
+        wq, wqs = {}, {}
+
+        def cast_w(a, b):
+            grp = ring.tile([P, PACK * KP], BF16, name="wgrp", align_bytes=64)
+            nc.scalar.copy(
+                out=grp[:].rearrange("p (t m j) -> p m j t", t=PACK, j=PACK),
+                in_=wraw[a, b][:].rearrange("p j (m t) -> p m j t", t=PACK),
+            )
+            wq[a, b] = held([P, KP], U32, "wq%d%d" % (a, b))
+            wqs[a, b] = held([P, KP], U8, "wqs%d%d" % (a, b))
+            nc.vector.quantize_mx(out=wq[a, b][:].bitcast(FP8X4), scales=wqs[a, b][:], in_=grp[:])
+
+        def first_stage(lhs, lhs_scale, rhs_planes, tag):
+            banks = [psum.tile([P, PACK * JT], F32, name=tag) for n in range(S // JT)]
+            for a in range(NPASS):
+                for n in range(S // JT):
+                    for t in range(PACK):
+                        nc.tensor.matmul_mx(
+                            out=banks[n][:, t * JT : (t + 1) * JT],
+                            lhsT=lhs(a, t),
+                            lhsT_scale=lhs_scale(a, t),
+                            rhs=vw[a][:, n * JT : (n + 1) * JT].bitcast(FP8X4),
+                            rhs_scale=rhs_planes(a, slice(n * JT, (n + 1) * JT)),
+                            start=(a == 0 and t == 0),
+                            stop=(a == NPASS - 1 and t == PACK - 1),
+                        )
+            return banks
+
+        xq, xqs, hq, hqs = {}, {}, {}, {}
+
+        def make_x(b):
+            banks = first_stage(
+                lambda a, t: wbw[:, 2 * (a * K + b * KP + t * P) : 2 * (a * K + b * KP + (t + 1) * P)].bitcast(FP4X4),
+                lambda a, t: wbs[:, a * K + b * KP + t * P : a * K + b * KP + (t + 1) * P],
+                lambda a, cols: (vs, vs_hi)[a][:, cols],
+                "acc_xb",
+            )
+            grp = held([P, S * PACK], BF16, "xgrp%d" % b)
+            for n in range(S // JT):
+                nc.vector.tensor_tensor(
+                    out=grp[:, n * JT * PACK : (n + 1) * JT * PACK].rearrange("p (j t) -> p j t", t=PACK),
+                    in0=banks[n][:].rearrange("p (t j) -> p j t", t=PACK),
+                    in1=g[:, b, :].unsqueeze(1).to_broadcast([P, JT, PACK]),
+                    op=ALU.mult,
+                )
+            xq[b] = held([P, S], U32, "xq%d" % b)
+            xqs[b] = held([P, S], U8, "xqs%d" % b)
+            nc.vector.quantize_mx(out=xq[b][:].bitcast(FP8X4), scales=xqs[b][:], in_=grp[:])
+
+        def make_h(b):
+            banks = first_stage(
+                lambda a, t: wq[a, b][:, t * P : (t + 1) * P].bitcast(FP8X4),
+                lambda a, t: wqs[a, b][:, t * P : (t + 1) * P],
+                lambda a, cols: vs[4 * a :, cols],
+                "acc_hef",
+            )
+            grp = held([P, S * PACK], BF16, "hgrp%d" % b)
+            for n in range(S // JT):
+                nc.scalar.activation(
+                    out=grp[:, n * JT * PACK : (n + 1) * JT * PACK].rearrange("p (j t) -> p j t", t=PACK),
+                    in_=banks[n][:].rearrange("p (t j) -> p j t", t=PACK),
+                    func=ACT.Abs,
+                )
+            hq[b] = held([P, S], U32, "hq%d" % b)
+            hqs[b] = held([P, S], U8, "hqs%d" % b)
+            nc.vector.quantize_mx(out=hq[b][:].bitcast(FP8X4), scales=hqs[b][:], in_=grp[:])
+
+        cast_w(0, 0)
+        cast_w(1, 0)
+        cast_w(0, 1)
+        make_h(0)
+        make_x(0)
+        cast_w(1, 1)
+        make_h(1)
+        make_x(1)
+        gather2_words(0)
+
+        w2q, w2qs = {}, {}
+
+        def cast_w2(c):
+            for b in range(NPASS):
+                grp = ring.tile([P, PACK * W2C], BF16, name="w2grp", align_bytes=64)
+                nc.scalar.copy(
+                    out=grp[:].rearrange("p (c i j) -> p c j i", i=4, j=PACK),
+                    in_=w2raw[c, b][:].rearrange("p j (c i) -> p c j i", i=4),
+                )
+                w2q[c, b] = held([P, W2C], U32, "w2q%d%d" % (c, b))
+                w2qs[c, b] = held([P, W2C], U8, "w2qs%d%d" % (c, b))
+                nc.vector.quantize_mx(out=w2q[c, b][:].bitcast(FP8X4), scales=w2qs[c, b][:], in_=grp[:])
+
+        def product(lhs, lhs_scale, rq, rqs, tag):
+            acc = psum.tile([P, S], F32, name=tag)
+            for a in range(NPASS):
+                nc.tensor.matmul_mx(
+                    out=acc[:],
+                    lhsT=lhs(a).bitcast(FP8X4),
+                    lhsT_scale=lhs_scale(a),
+                    rhs=rq[a][:].bitcast(FP8X4),
+                    rhs_scale=rqs[a][:],
+                    start=(a == 0),
+                    stop=(a == NPASS - 1),
+                )
+            return acc
+
+        for c in range(S2 // W2C):
+            cast_w2(c)
+            if c + 1 < S2 // GC:
+                gather2_words(c + 1)
+            for u in range(2):
+                cols = slice(u * P, (u + 1) * P)
+                v2_words = lambda a: v2w[c, a][:, cols]
+                v2_scale = lambda a: v2s[c][4 * a :, cols]
+                acc_b = product(v2_words, v2_scale, xq, xqs, "acc_xb")
+                acc_e = product(v2_words, v2_scale, hq, hqs, "acc_hef")
+                acc_f = product(lambda a: w2q[c, a][:, cols], lambda a: w2qs[c, a][:, cols], hq, hqs, "acc_hef")
+                b_sb = ring.tile([P, S], F32, name="b_sb", bufs=6)
+                nc.scalar.copy(out=b_sb[:], in_=acc_b[:])
+                top = ring.tile([P, S], F32, name="top")
+                nc.vector.tensor_tensor(out=top[:], in0=acc_f[:], in1=b_sb[:], op=ALU.max)
+                diff = ring.tile([P, S], F32, name="diff")
+                nc.vector.tensor_tensor(out=diff[:], in0=acc_e[:], in1=top[:], op=ALU.subtract)
+                res = ring.tile([P, S], F32, name="res")
+                nc.gpsimd.tensor_tensor(out=res[:], in0=diff[:], in1=seat_t[c][:, u, :], op=ALU.mult)
+                m0 = c * W2C + u * P
+                nc.sync.dma_start(out=out[m0 : m0 + P, :], in_=res[:])

@@ -22,7 +22,7 @@ KP = P * PACK
 NPASS = K // KP
 JT = 128
 W2C = 256
-GC = 256
+GC = 512
 
 
 def tile_list_table_companion_ease_kernel(
@@ -32,11 +32,13 @@ def tile_list_table_companion_ease_kernel(
     with ExitStack() as ctx:
         keep = ctx.enter_context(tc.tile_pool(name="keep", bufs=1))
         ring = ctx.enter_context(tc.tile_pool(name="ring", bufs=3))
-        ring2 = ctx.enter_context(tc.tile_pool(name="ring2", bufs=2))
-        psum = ctx.enter_context(tc.psum_pool(name="psum", bufs=4))
+        psum = ctx.enter_context(tc.psum_pool(name="psum", bufs=1))
 
-        def held(shape, dtype, name):
-            return keep.tile(shape, dtype, name=name, align_bytes=64)
+        def held(shape, dtype, name, tag=None):
+            return keep.tile(shape, dtype, name=name, tag=tag or name, align_bytes=64)
+
+        def bank(n):
+            return psum.tile([P, S], F32, name="bank%d" % n, tag="bank%d" % n)
 
         o1 = keep.tile([P, S // 16], U16, name="o1")
         o2 = keep.tile([P, S2 // 16], U16, name="o2")
@@ -47,13 +49,11 @@ def tile_list_table_companion_ease_kernel(
 
         tw = [held([P, T], U32, "tw%d" % a) for a in range(NPASS)]
         wraw = {}
-        for a in range(NPASS):
-            for b in range(NPASS):
-                wraw[a, b] = held([P, PACK, KP], F32, "wraw%d%d" % (a, b))
-        wbw_raw = held([P, NPASS, 2 * K], U8, "wbw_raw")
+        wbw_raw = held([P, NPASS * 2 * K], U8, "wbw_raw", "stage2")
         g = held([P, NPASS, PACK], F32, "g")
 
-        def load_w(a, b):
+        def load_w(a, b, tag):
+            wraw[a, b] = held([P, PACK, KP], F32, "wraw%d%d" % (a, b), tag)
             nc.sync.dma_start(
                 out=wraw[a, b][:],
                 in_=w[a * KP : (a + 1) * KP, b * KP : (b + 1) * KP].rearrange("(p j) c -> p j c", j=PACK),
@@ -77,82 +77,77 @@ def tile_list_table_companion_ease_kernel(
                 out=sc_both[:].bitcast(I32)[32 * q : 32 * q + 8, :],
                 in_=ts32[:, 4 * q : 4 * q + 4, :],
             )
-        load_w(0, 0)
-        load_tab(0)
-        load_w(1, 0)
-        load_tab(1)
+        load_w(0, 0, "stage0")
         for q in range(4):
             nc.sync.dma_start(
                 out=wbs_raw[:].bitcast(I32)[32 * q : 32 * q + 4, :].rearrange("r (a c) -> r a c", a=NPASS),
                 in_=ws32[:, 4 * q : 4 * q + 4, :].rearrange("a r c -> r a c"),
             )
         nc.sync.dma_start(
-            out=wbw_raw[:].rearrange("p a c -> p (a c)").bitcast(I32).rearrange("p (a c) -> p a c", a=NPASS),
+            out=wbw_raw[:].bitcast(I32).rearrange("p (a c) -> p a c", a=NPASS),
             in_=wb_words.bitcast(I32).rearrange("a p c -> p a c"),
         )
-        load_w(0, 1)
-        load_w(1, 1)
+        load_tab(0)
+        load_w(1, 0, "stage1")
+        load_tab(1)
 
         w2raw = {}
         seat_t = {}
-        for c in range(S2 // W2C):
+
+        def load_w2(half, tag):
+            tile = held([P, NPASS * PACK * KP], F32, "w2raw%d" % half, tag)
             for b in range(NPASS):
-                w2raw[c, b] = held([P, PACK, W2C], F32, "w2raw%d%d" % (c, b))
+                w2raw[half, b] = tile[:, b * PACK * KP : (b + 1) * PACK * KP].rearrange("p (j c) -> p j c", j=PACK)
                 nc.sync.dma_start(
-                    out=w2raw[c, b][:],
-                    in_=w2[b * KP : (b + 1) * KP, c * W2C : (c + 1) * W2C].rearrange("(p j) c -> p j c", j=PACK),
+                    out=w2raw[half, b],
+                    in_=w2[b * KP : (b + 1) * KP, half * KP : (half + 1) * KP].rearrange("(p j) c -> p j c", j=PACK),
                 )
-            if c > 0:
-                seat_t[c - 1] = held([P, 2, S], F32, "seat%d" % (c - 1))
-                nc.sync.dma_start(
-                    out=seat_t[c - 1][:],
-                    in_=seat[(c - 1) * W2C : c * W2C, :].rearrange("(u p) j -> p u j", p=P),
-                )
-        c = S2 // W2C - 1
-        seat_t[c] = held([P, 2, S], F32, "seat%d" % c)
-        nc.sync.dma_start(
-            out=seat_t[c][:], in_=seat[c * W2C : (c + 1) * W2C, :].rearrange("(u p) j -> p u j", p=P)
-        )
+
+        def load_seat(half, tag):
+            seat_t[half] = held([P, 4, S], F32, "seat%d" % half, tag)
+            nc.sync.dma_start(
+                out=seat_t[half][:],
+                in_=seat[half * KP : (half + 1) * KP, :].rearrange("(u p) j -> p u j", p=P),
+            )
 
         vs = held([P, S], U8, "vs")
         vw = [held([P, S], U32, "vw%d" % a) for a in range(NPASS)]
         nc.vector.tensor_copy(vs[:], sc_both[:].indirect(o1[:]))
         for q in range(4):
-            nc.gpsimd.dma_start(
+            nc.sync.dma_start(
                 out=vs_hi[:].bitcast(I32)[32 * q : 32 * q + 4, :],
                 in_=vs[:].bitcast(I32)[32 * q + 4 : 32 * q + 8, :],
             )
-        v2s = [held([P, GC], U8, "v2s%d" % c) for c in range(S2 // GC)]
+        v2s = held([P, S2], U8, "v2s")
+        nc.vector.tensor_copy(v2s[:], sc_both[:].indirect(o2[:]))
+        nc.vector.tensor_copy(vw[0][:], tw[0][:].indirect(o1[:]))
         v2w = {}
 
-        def gather2_scales(c):
-            nc.vector.tensor_copy(v2s[c][:], sc_both[:].indirect(o2[:, c * GC // 16 : (c + 1) * GC // 16]))
+        def gather2_words(a, tile):
+            v2w[a] = tile
+            for c in range(S2 // GC):
+                nc.vector.tensor_copy(
+                    tile[:, c * GC : (c + 1) * GC], tw[a][:].indirect(o2[:, c * GC // 16 : (c + 1) * GC // 16])
+                )
 
-        def gather2_words(c):
-            for a in range(NPASS):
-                v2w[c, a] = ring2.tile([P, GC], U32, name="v2w%d" % a, align_bytes=64)
-                nc.vector.tensor_copy(v2w[c, a][:], tw[a][:].indirect(o2[:, c * GC // 16 : (c + 1) * GC // 16]))
-
-        for c in range(S2 // GC):
-            gather2_scales(c)
-        nc.vector.tensor_copy(vw[0][:], tw[0][:].indirect(o1[:]))
-
+        nc.vector.tensor_copy(vw[1][:], tw[1][:].indirect(o1[:]))
         wbs = held([P, NPASS * K], U8, "wbs")
         wbw = held([P, NPASS * 2 * K], U8, "wbw")
-        nc.vector.tensor_copy(
-            out=wbs[:].rearrange("p (u t m) -> p u m t", t=PACK, m=P),
-            in_=wbs_raw[:].rearrange("p (u m t) -> p u m t", t=PACK, m=P),
-        )
-        nc.vector.tensor_copy(vw[1][:], tw[1][:].indirect(o1[:]))
-        nc.vector.tensor_copy(
-            out=wbw[:].bitcast(U16).rearrange("p (u t m) -> p u m t", t=PACK, m=P),
-            in_=wbw_raw[:].rearrange("p a c -> p (a c)").bitcast(U16).rearrange("p (u m t) -> p u m t", t=PACK, m=P),
-        )
+
+        def deal_wb():
+            nc.vector.tensor_copy(
+                out=wbs[:].rearrange("p (u t m) -> p u t m", t=PACK, m=P),
+                in_=wbs_raw[:].rearrange("p (u m t) -> p u t m", t=PACK, m=P),
+            )
+            nc.scalar.copy(
+                out=wbw[:].bitcast(U16).rearrange("p (u t m) -> p u t m", t=PACK, m=P),
+                in_=wbw_raw[:].bitcast(U16).rearrange("p (u m t) -> p u t m", t=PACK, m=P),
+            )
 
         wq, wqs = {}, {}
 
         def cast_w(a, b):
-            grp = ring.tile([P, PACK * KP], BF16, name="wgrp", align_bytes=64)
+            grp = held([P, PACK * KP], BF16, "wgrp%d%d" % (a, b))
             nc.scalar.copy(
                 out=grp[:].rearrange("p (t m j) -> p m j t", t=PACK, j=PACK),
                 in_=wraw[a, b][:].rearrange("p j (m t) -> p m j t", t=PACK),
@@ -161,8 +156,8 @@ def tile_list_table_companion_ease_kernel(
             wqs[a, b] = held([P, KP], U8, "wqs%d%d" % (a, b))
             nc.vector.quantize_mx(out=wq[a, b][:].bitcast(FP8X4), scales=wqs[a, b][:], in_=grp[:])
 
-        def first_stage(lhs, lhs_scale, rhs_planes, tag):
-            banks = [psum.tile([P, PACK * JT], F32, name=tag) for n in range(S // JT)]
+        def first_stage(lhs, lhs_scale, rhs_planes, first_bank):
+            banks = [bank(first_bank + n) for n in range(S // JT)]
             for a in range(NPASS):
                 for n in range(S // JT):
                     for t in range(PACK):
@@ -184,7 +179,7 @@ def tile_list_table_companion_ease_kernel(
                 lambda a, t: wbw[:, 2 * (a * K + b * KP + t * P) : 2 * (a * K + b * KP + (t + 1) * P)].bitcast(FP4X4),
                 lambda a, t: wbs[:, a * K + b * KP + t * P : a * K + b * KP + (t + 1) * P],
                 lambda a, cols: (vs, vs_hi)[a][:, cols],
-                "acc_xb",
+                0,
             )
             grp = held([P, S * PACK], BF16, "xgrp%d" % b)
             for n in range(S // JT):
@@ -203,7 +198,7 @@ def tile_list_table_companion_ease_kernel(
                 lambda a, t: wq[a, b][:, t * P : (t + 1) * P].bitcast(FP8X4),
                 lambda a, t: wqs[a, b][:, t * P : (t + 1) * P],
                 lambda a, cols: vs[4 * a :, cols],
-                "acc_hef",
+                4,
             )
             grp = held([P, S * PACK], BF16, "hgrp%d" % b)
             for n in range(S // JT):
@@ -217,30 +212,40 @@ def tile_list_table_companion_ease_kernel(
             nc.vector.quantize_mx(out=hq[b][:].bitcast(FP8X4), scales=hqs[b][:], in_=grp[:])
 
         cast_w(0, 0)
+        load_w(0, 1, "stage0")
         cast_w(1, 0)
+        deal_wb()
+        load_w(1, 1, "stage2")
+        load_w2(0, "stage1")
         cast_w(0, 1)
-        make_h(0)
-        make_x(0)
+        load_w2(1, "stage0")
         cast_w(1, 1)
+        load_seat(0, "stage2")
+        load_seat(1, "wgrp11")
+        make_h(0)
         make_h(1)
+        make_x(0)
         make_x(1)
-        gather2_words(0)
+        gather2_words(0, held([P, S2], U32, "v2w0"))
+        gather2_words(1, held([P, S2], U32, "v2w1", "wgrp10"))
 
         w2q, w2qs = {}, {}
 
         def cast_w2(c):
+            grp = held([P, NPASS * PACK * W2C], BF16, "w2grp%d" % c, "xgrp1" if c == 0 else None)
+            copy = nc.vector.tensor_copy if c == 0 else nc.scalar.copy
+            c0 = c * W2C % KP
             for b in range(NPASS):
-                grp = ring.tile([P, PACK * W2C], BF16, name="w2grp", align_bytes=64)
-                nc.scalar.copy(
-                    out=grp[:].rearrange("p (c i j) -> p c j i", i=4, j=PACK),
-                    in_=w2raw[c, b][:].rearrange("p j (c i) -> p c j i", i=4),
+                copy(
+                    out=grp[:, b * PACK * W2C : (b + 1) * PACK * W2C].rearrange("p (c i j) -> p c j i", i=4, j=PACK),
+                    in_=w2raw[c * W2C // KP, b][:, :, c0 : c0 + W2C].rearrange("p j (c i) -> p c j i", i=4),
                 )
-                w2q[c, b] = held([P, W2C], U32, "w2q%d%d" % (c, b))
-                w2qs[c, b] = held([P, W2C], U8, "w2qs%d%d" % (c, b))
-                nc.vector.quantize_mx(out=w2q[c, b][:].bitcast(FP8X4), scales=w2qs[c, b][:], in_=grp[:])
+            w2q[c] = held([P, NPASS * W2C], U32, "w2q%d" % c)
+            w2qs[c] = held([P, NPASS * W2C], U8, "w2qs%d" % c)
+            nc.vector.quantize_mx(out=w2q[c][:].bitcast(FP8X4), scales=w2qs[c][:], in_=grp[:])
 
-        def product(lhs, lhs_scale, rq, rqs, tag):
-            acc = psum.tile([P, S], F32, name=tag)
+        def product(lhs, lhs_scale, rq, rqs, n):
+            acc = bank(n)
             for a in range(NPASS):
                 nc.tensor.matmul_mx(
                     out=acc[:],
@@ -253,24 +258,34 @@ def tile_list_table_companion_ease_kernel(
                 )
             return acc
 
+        def with_v2(m, rq, rqs, n):
+            cols = slice(m * P, (m + 1) * P)
+            return product(lambda a: v2w[a][:, cols], lambda a: v2s[4 * a :, cols], rq, rqs, n)
+
+        def with_w2(m, n):
+            c, u = divmod(m, 2)
+            cols = lambda a: slice(a * W2C + u * P, a * W2C + (u + 1) * P)
+            return product(lambda a: w2q[c][:, cols(a)], lambda a: w2qs[c][:, cols(a)], hq, hqs, n)
+
         for c in range(S2 // W2C):
             cast_w2(c)
-            if c + 1 < S2 // GC:
-                gather2_words(c + 1)
-            for u in range(2):
-                cols = slice(u * P, (u + 1) * P)
-                v2_words = lambda a: v2w[c, a][:, cols]
-                v2_scale = lambda a: v2s[c][4 * a :, cols]
-                acc_b = product(v2_words, v2_scale, xq, xqs, "acc_xb")
-                acc_e = product(v2_words, v2_scale, hq, hqs, "acc_hef")
-                acc_f = product(lambda a: w2q[c, a][:, cols], lambda a: w2qs[c, a][:, cols], hq, hqs, "acc_hef")
-                b_sb = ring.tile([P, S], F32, name="b_sb", bufs=6)
-                nc.scalar.copy(out=b_sb[:], in_=acc_b[:])
-                top = ring.tile([P, S], F32, name="top")
-                nc.vector.tensor_tensor(out=top[:], in0=acc_f[:], in1=b_sb[:], op=ALU.max)
-                diff = ring.tile([P, S], F32, name="diff")
-                nc.vector.tensor_tensor(out=diff[:], in0=acc_e[:], in1=top[:], op=ALU.subtract)
-                res = ring.tile([P, S], F32, name="res")
-                nc.gpsimd.tensor_tensor(out=res[:], in0=diff[:], in1=seat_t[c][:, u, :], op=ALU.mult)
-                m0 = c * W2C + u * P
-                nc.sync.dma_start(out=out[m0 : m0 + P, :], in_=res[:])
+            pair = (2 * c, 2 * c + 1)
+            b_sb, acc_f, acc_e, top = {}, {}, {}, {}
+            for m in pair:
+                acc_b = with_v2(m, xq, xqs, m % 2)
+                b_sb[m] = held([P, S], F32, "b_sb%d" % m)
+                nc.scalar.copy(out=b_sb[m][:], in_=acc_b[:])
+            for m in pair:
+                acc_f[m] = with_w2(m, 2 + m % 3)
+            for m in pair:
+                acc_e[m] = with_v2(m, hq, hqs, 5 + m % 3)
+            for m in pair:
+                top[m] = ring.tile([P, S], F32, name="top")
+                nc.vector.tensor_tensor(out=top[m][:], in0=acc_f[m][:], in1=b_sb[m][:], op=ALU.max)
+            for m in pair:
+                diff = ring.tile([P, S], F32, name="diff", bufs=4)
+                nc.vector.tensor_tensor(out=diff[:], in0=acc_e[m][:], in1=top[m][:], op=ALU.subtract)
+                res = ring.tile([P, S], F32, name="res", bufs=4)
+                eng = nc.vector if m == S2 // P - 1 else nc.gpsimd
+                eng.tensor_tensor(out=res[:], in0=diff[:], in1=seat_t[m // 4][:, m % 4, :], op=ALU.mult)
+                nc.sync.dma_start(out=out[m * P : (m + 1) * P, :], in_=res[:])

@@ -42,7 +42,7 @@ def tile_list_table_companion_ease_kernel(
 
         o1 = keep.tile([P, S // 16], U16, name="o1")
         o2 = keep.tile([P, S2 // 16], U16, name="o2")
-        sc_both = held([P, T], U8, "sc_both")
+        sc_both = held([P, T], U8, "sc_both", "stage1")
         wbs_raw = held([P, NPASS * K], U8, "wbs_raw")
         nc.vector.memset(sc_both[:].bitcast(I32), 0)
         nc.gpsimd.memset(wbs_raw[:].bitcast(I32), 0)
@@ -77,6 +77,7 @@ def tile_list_table_companion_ease_kernel(
                 out=sc_both[:].bitcast(I32)[32 * q : 32 * q + 8, :],
                 in_=ts32[:, 4 * q : 4 * q + 4, :],
             )
+        load_tab(0)
         load_w(0, 0, "stage0")
         for q in range(4):
             nc.sync.dma_start(
@@ -87,8 +88,6 @@ def tile_list_table_companion_ease_kernel(
             out=wbw_raw[:].bitcast(I32).rearrange("p (a c) -> p a c", a=NPASS),
             in_=wb_words.bitcast(I32).rearrange("a p c -> p a c"),
         )
-        load_tab(0)
-        load_w(1, 0, "stage1")
         load_tab(1)
 
         w2raw = {}
@@ -120,6 +119,7 @@ def tile_list_table_companion_ease_kernel(
             )
         v2s = held([P, S2], U8, "v2s")
         nc.vector.tensor_copy(v2s[:], sc_both[:].indirect(o2[:]))
+        load_w(1, 0, "stage1")
         nc.vector.tensor_copy(vw[0][:], tw[0][:].indirect(o1[:]))
         v2w = {}
 
@@ -221,19 +221,19 @@ def tile_list_table_companion_ease_kernel(
         load_w2(1, "stage0")
         cast_w(1, 1)
         load_seat(0, "stage2")
-        load_seat(1, "wgrp11")
         make_h(0)
+        load_seat(1, "hgrp0")
         make_h(1)
         make_x(0)
         make_x(1)
         gather2_words(0, held([P, S2], U32, "v2w0"))
-        gather2_words(1, held([P, S2], U32, "v2w1", "wgrp10"))
+        gather2_words(1, held([P, S2], U32, "v2w1"))
 
         w2q, w2qs = {}, {}
 
         def cast_w2(c):
-            grp = held([P, NPASS * PACK * W2C], BF16, "w2grp%d" % c, "xgrp1" if c == 0 else None)
-            copy = nc.vector.tensor_copy if c == 0 else nc.scalar.copy
+            grp = held([P, NPASS * PACK * W2C], BF16, "w2grp%d" % c, "xgrp%d" % (1 - c) if c < 2 else None)
+            copy = nc.vector.tensor_copy if c < 2 else nc.scalar.copy
             c0 = c * W2C % KP
             for b in range(NPASS):
                 copy(
@@ -267,25 +267,35 @@ def tile_list_table_companion_ease_kernel(
             cols = lambda a: slice(a * W2C + u * P, a * W2C + (u + 1) * P)
             return product(lambda a: w2q[c][:, cols(a)], lambda a: w2qs[c][:, cols(a)], hq, hqs, n)
 
+        b_sb = {}
+
+        def make_b(m):
+            acc_b = with_v2(m, xq, xqs, m % 4)
+            b_sb[m] = held([P, S], F32, "b_sb%d" % m)
+            nc.scalar.copy(out=b_sb[m][:], in_=acc_b[:])
+
+        for m in range(2):
+            make_b(m)
+        cast_w2(0)
         for c in range(S2 // W2C):
-            cast_w2(c)
             pair = (2 * c, 2 * c + 1)
-            b_sb, acc_f, acc_e, top = {}, {}, {}, {}
+            acc_f, acc_e, top, diff = {}, {}, {}, {}
             for m in pair:
-                acc_b = with_v2(m, xq, xqs, m % 2)
-                b_sb[m] = held([P, S], F32, "b_sb%d" % m)
-                nc.scalar.copy(out=b_sb[m][:], in_=acc_b[:])
+                acc_f[m] = with_w2(m, 4 + m % 2)
             for m in pair:
-                acc_f[m] = with_w2(m, 2 + m % 3)
-            for m in pair:
-                acc_e[m] = with_v2(m, hq, hqs, 5 + m % 3)
+                acc_e[m] = with_v2(m, hq, hqs, 6 + m % 2)
+            if c + 1 < S2 // W2C:
+                cast_w2(c + 1)
+                for m in pair:
+                    make_b(m + 2)
             for m in pair:
                 top[m] = ring.tile([P, S], F32, name="top")
                 nc.vector.tensor_tensor(out=top[m][:], in0=acc_f[m][:], in1=b_sb[m][:], op=ALU.max)
             for m in pair:
-                diff = ring.tile([P, S], F32, name="diff", bufs=4)
-                nc.vector.tensor_tensor(out=diff[:], in0=acc_e[m][:], in1=top[m][:], op=ALU.subtract)
+                diff[m] = ring.tile([P, S], F32, name="diff", bufs=4)
+                nc.vector.tensor_tensor(out=diff[m][:], in0=acc_e[m][:], in1=top[m][:], op=ALU.subtract)
+            for m in pair:
                 res = ring.tile([P, S], F32, name="res", bufs=4)
-                eng = nc.vector if m == S2 // P - 1 else nc.gpsimd
-                eng.tensor_tensor(out=res[:], in0=diff[:], in1=seat_t[m // 4][:, m % 4, :], op=ALU.mult)
+                eng = nc.vector if c == S2 // W2C - 1 else nc.gpsimd
+                eng.tensor_tensor(out=res[:], in0=diff[m][:], in1=seat_t[m // 4][:, m % 4, :], op=ALU.mult)
                 nc.sync.dma_start(out=out[m * P : (m + 1) * P, :], in_=res[:])

@@ -148,10 +148,13 @@ def tile_list_table_companion_ease_kernel(
 
         def cast_w(a, b):
             grp = held([P, PACK * KP], BF16, "wgrp%d%d" % (a, b))
-            nc.scalar.copy(
-                out=grp[:].rearrange("p (t m j) -> p m j t", t=PACK, j=PACK),
-                in_=wraw[a, b][:].rearrange("p j (m t) -> p m j t", t=PACK),
-            )
+            dst = grp[:].rearrange("p (t m j) -> p m j t", t=PACK, j=PACK)
+            src = wraw[a, b][:].rearrange("p j (m t) -> p m j t", t=PACK)
+            if b == 0:
+                nc.scalar.copy(out=dst, in_=src)
+            else:
+                nc.scalar.copy(out=dst[:, :, :, 0:2], in_=src[:, :, :, 0:2])
+                nc.vector.tensor_copy(out=dst[:, :, :, 2:4], in_=src[:, :, :, 2:4])
             wq[a, b] = held([P, KP], U32, "wq%d%d" % (a, b))
             wqs[a, b] = held([P, KP], U8, "wqs%d%d" % (a, b))
             nc.vector.quantize_mx(out=wq[a, b][:].bitcast(FP8X4), scales=wqs[a, b][:], in_=grp[:])

from contextlib import ExitStack

import concourse.mybir as mybir

K, T, S, S2 = 1024, 2048, 512, 1024
FLOPS = 2 * K * K * S * 2 + 2 * K * S2 * S * 3

F32 = mybir.dt.float32
BF16 = mybir.dt.bfloat16
I32 = mybir.dt.int32
U32 = mybir.dt.uint32
U16 = mybir.dt.uint16
U8 = mybir.dt.uint8
FP8X4 = mybir.dt.float8_e4m3fn_x4
FP4X4 = mybir.dt.float4_e2m1fn_x4
ALU = mybir.AluOpType
ACT = mybir.ActivationFunctionType

P = 128
PACK = 4
KP = P * PACK
NPASS = K // KP
JT = 128
W2C = 256
GC = 512


def tile_list_table_companion_ease_kernel(
    tc, tab_words, tab_scales, offs, offs2, w, wb_words, wb_scales, gain, w2, seat, out
):
    nc = tc.nc
    with ExitStack() as ctx:
        keep = ctx.enter_context(tc.tile_pool(name="keep", bufs=1))
        ring = ctx.enter_context(tc.tile_pool(name="ring", bufs=3))
        psum = ctx.enter_context(tc.psum_pool(name="psum", bufs=1))

        def held(shape, dtype, name, tag=None):
            return keep.tile(shape, dtype, name=name, tag=tag or name, align_bytes=64)

        def bank(n):
            return psum.tile([P, S], F32, name="bank%d" % n, tag="bank%d" % n)

        o1 = keep.tile([P, S // 16], U16, name="o1")
        o2 = keep.tile([P, S2 // 16], U16, name="o2")
        sc_both = held([P, T], U8, "sc_both", "stage1")
        wbs_raw = held([P, NPASS * K], U8, "wbs_raw")
        nc.vector.memset(sc_both[:].bitcast(I32), 0)
        nc.gpsimd.memset(wbs_raw[:].bitcast(I32), 0)

        tw = [held([P, T], U32, "tw%d" % a) for a in range(NPASS)]
        wraw = {}
        wbw_raw = held([P, NPASS * 2 * K], U8, "wbw_raw", "stage2")
        g = held([P, NPASS, PACK], F32, "g")

        def load_w(a, b, tag):
            wraw[a, b] = held([P, PACK, KP], F32, "wraw%d%d" % (a, b), tag)
            nc.sync.dma_start(
                out=wraw[a, b][:],
                in_=w[a * KP : (a + 1) * KP, b * KP : (b + 1) * KP].rearrange("(p j) c -> p j c", j=PACK),
            )

        def load_tab(a):
            nc.sync.dma_start(
                out=tw[a][:].bitcast(I32),
                in_=tab_words[a].rearrange("p t i -> p (t i)").bitcast(I32),
            )

        vs_hi = held([P, S], U8, "vs_hi")
        nc.gpsimd.memset(vs_hi[:].bitcast(I32), 0)
        ts32 = tab_scales.bitcast(I32)
        ws32 = wb_scales.bitcast(I32)
        nc.sync.dma_start(o1[:], offs)
        nc.sync.dma_start(o2[:], offs2)
        nc.sync.dma_start(out=g[:], in_=gain.rearrange("(b p t) -> p b t", b=NPASS, t=PACK))
        for q in range(4):
            nc.sync.dma_start(
                out=sc_both[:].bitcast(I32)[32 * q : 32 * q + 8, :],
                in_=ts32[:, 4 * q : 4 * q + 4, :],
            )
        load_tab(0)
        load_w(0, 0, "stage0")
        for q in range(4):
            nc.sync.dma_start(
                out=wbs_raw[:].bitcast(I32)[32 * q : 32 * q + 4, :].rearrange("r (a c) -> r a c", a=NPASS),
                in_=ws32[:, 4 * q : 4 * q + 4, :].rearrange("a r c -> r a c"),
            )
        nc.sync.dma_start(
            out=wbw_raw[:].bitcast(I32).rearrange("p (a c) -> p a c", a=NPASS),
            in_=wb_words.bitcast(I32).rearrange("a p c -> p a c"),
        )
        load_tab(1)

        w2raw = {}
        seat_t = {}

        def load_w2(half, tag):
            tile = held([P, NPASS * PACK * KP], F32, "w2raw%d" % half, tag)
            for b in range(NPASS):
                w2raw[half, b] = tile[:, b * PACK * KP : (b + 1) * PACK * KP].rearrange("p (j c) -> p j c", j=PACK)
                nc.sync.dma_start(
                    out=w2raw[half, b],
                    in_=w2[b * KP : (b + 1) * KP, half * KP : (half + 1) * KP].rearrange("(p j) c -> p j c", j=PACK),
                )

        def load_seat(half, tag):
            seat_t[half] = held([P, 4, S], F32, "seat%d" % half, tag)
            nc.sync.dma_start(
                out=seat_t[half][:],
                in_=seat[half * KP : (half + 1) * KP, :].rearrange("(u p) j -> p u j", p=P),
            )

        vs = held([P, S], U8, "vs")
        vw = [held([P, S], U32, "vw%d" % a) for a in range(NPASS)]
        nc.vector.tensor_copy(vs[:], sc_both[:].indirect(o1[:]))
        for q in range(4):
            nc.sync.dma_start(
                out=vs_hi[:].bitcast(I32)[32 * q : 32 * q + 4, :],
                in_=vs[:].bitcast(I32)[32 * q + 4 : 32 * q + 8, :],
            )
        v2s = held([P, S2], U8, "v2s")
        nc.vector.tensor_copy(v2s[:], sc_both[:].indirect(o2[:]))
        load_w(1, 0, "stage1")
        nc.vector.tensor_copy(vw[0][:], tw[0][:].indirect(o1[:]))
        v2w = {}

        def gather2_words(a, tile):
            v2w[a] = tile
            for c in range(S2 // GC):
                nc.vector.tensor_copy(
                    tile[:, c * GC : (c + 1) * GC], tw[a][:].indirect(o2[:, c * GC // 16 : (c + 1) * GC // 16])
                )

        nc.vector.tensor_copy(vw[1][:], tw[1][:].indirect(o1[:]))
        wbs = held([P, NPASS * K], U8, "wbs")
        wbw = held([P, NPASS * 2 * K], U8, "wbw")

        def deal_wb():
            nc.vector.tensor_copy(
                out=wbs[:].rearrange("p (u t m) -> p u t m", t=PACK, m=P),
                in_=wbs_raw[:].rearrange("p (u m t) -> p u t m", t=PACK, m=P),
            )
            nc.scalar.copy(
                out=wbw[:].bitcast(U16).rearrange("p (u t m) -> p u t m", t=PACK, m=P),
                in_=wbw_raw[:].bitcast(U16).rearrange("p (u m t) -> p u t m", t=PACK, m=P),
            )

        wq, wqs = {}, {}

        def cast_w(a, b):
            grp = held([P, PACK * KP], BF16, "wgrp%d%d" % (a, b))
            dst = grp[:].rearrange("p (t m j) -> p m j t", t=PACK, j=PACK)
            src = wraw[a, b][:].rearrange("p j (m t) -> p m j t", t=PACK)
            if b == 0:
                nc.scalar.copy(out=dst, in_=src)
            else:
                nc.scalar.copy(out=dst[:, :, :, 0:2], in_=src[:, :, :, 0:2])
                nc.vector.tensor_copy(out=dst[:, :, :, 2:4], in_=src[:, :, :, 2:4])
            wq[a, b] = held([P, KP], U32, "wq%d%d" % (a, b))
            wqs[a, b] = held([P, KP], U8, "wqs%d%d" % (a, b))
            nc.vector.quantize_mx(out=wq[a, b][:].bitcast(FP8X4), scales=wqs[a, b][:], in_=grp[:])

        def first_stage(lhs, lhs_scale, rhs_planes, first_bank):
            banks = [bank(first_bank + n) for n in range(S // JT)]
            for a in range(NPASS):
                for n in range(S // JT):
                    for t in range(PACK):
                        nc.tensor.matmul_mx(
                            out=banks[n][:, t * JT : (t + 1) * JT],
                            lhsT=lhs(a, t),
                            lhsT_scale=lhs_scale(a, t),
                            rhs=vw[a][:, n * JT : (n + 1) * JT].bitcast(FP8X4),
                            rhs_scale=rhs_planes(a, slice(n * JT, (n + 1) * JT)),
                            start=(a == 0 and t == 0),
                            stop=(a == NPASS - 1 and t == PACK - 1),
                        )
            return banks

        xq, xqs, hq, hqs = {}, {}, {}, {}

        def make_x(b):
            banks = first_stage(
                lambda a, t: wbw[:, 2 * (a * K + b * KP + t * P) : 2 * (a * K + b * KP + (t + 1) * P)].bitcast(FP4X4),
                lambda a, t: wbs[:, a * K + b * KP + t * P : a * K + b * KP + (t + 1) * P],
                lambda a, cols: (vs, vs_hi)[a][:, cols],
                0,
            )
            grp = held([P, S * PACK], BF16, "xgrp%d" % b)
            for n in range(S // JT):
                nc.vector.tensor_tensor(
                    out=grp[:, n * JT * PACK : (n + 1) * JT * PACK].rearrange("p (j t) -> p j t", t=PACK),
                    in0=banks[n][:].rearrange("p (t j) -> p j t", t=PACK),
                    in1=g[:, b, :].unsqueeze(1).to_broadcast([P, JT, PACK]),
                    op=ALU.mult,
                )
            xq[b] = held([P, S], U32, "xq%d" % b)
            xqs[b] = held([P, S], U8, "xqs%d" % b)
            nc.vector.quantize_mx(out=xq[b][:].bitcast(FP8X4), scales=xqs[b][:], in_=grp[:])

        def make_h(b):
            banks = first_stage(
                lambda a, t: wq[a, b][:, t * P : (t + 1) * P].bitcast(FP8X4),
                lambda a, t: wqs[a, b][:, t * P : (t + 1) * P],
                lambda a, cols: vs[4 * a :, cols],
                4,
            )
            grp = held([P, S * PACK], BF16, "hgrp%d" % b)
            for n in range(S // JT):
                nc.scalar.activation(
                    out=grp[:, n * JT * PACK : (n + 1) * JT * PACK].rearrange("p (j t) -> p j t", t=PACK),
                    in_=banks[n][:].rearrange("p (t j) -> p j t", t=PACK),
                    func=ACT.Abs,
                )
            hq[b] = held([P, S], U32, "hq%d" % b)
            hqs[b] = held([P, S], U8, "hqs%d" % b)
            nc.vector.quantize_mx(out=hq[b][:].bitcast(FP8X4), scales=hqs[b][:], in_=grp[:])

        cast_w(0, 0)
        load_w(0, 1, "stage0")
        cast_w(1, 0)
        deal_wb()
        load_w(1, 1, "stage2")
        load_w2(0, "stage1")
        cast_w(0, 1)
        load_w2(1, "stage0")
        cast_w(1, 1)
        load_seat(0, "stage2")
        make_h(0)
        load_seat(1, "hgrp0")
        make_h(1)
        make_x(0)
        make_x(1)
        gather2_words(0, held([P, S2], U32, "v2w0"))
        gather2_words(1, held([P, S2], U32, "v2w1"))

        w2q, w2qs = {}, {}

        def cast_w2(c):
            grp = held([P, NPASS * PACK * W2C], BF16, "w2grp%d" % c, "xgrp%d" % (1 - c) if c < 2 else None)
            copy = nc.vector.tensor_copy if c < 2 else nc.scalar.copy
            c0 = c * W2C % KP
            for b in range(NPASS):
                copy(
                    out=grp[:, b * PACK * W2C : (b + 1) * PACK * W2C].rearrange("p (c i j) -> p c j i", i=4, j=PACK),
                    in_=w2raw[c * W2C // KP, b][:, :, c0 : c0 + W2C].rearrange("p j (c i) -> p c j i", i=4),
                )
            w2q[c] = held([P, NPASS * W2C], U32, "w2q%d" % c)
            w2qs[c] = held([P, NPASS * W2C], U8, "w2qs%d" % c)
            nc.vector.quantize_mx(out=w2q[c][:].bitcast(FP8X4), scales=w2qs[c][:], in_=grp[:])

        def product(lhs, lhs_scale, rq, rqs, n):
            acc = bank(n)
            for a in range(NPASS):
                nc.tensor.matmul_mx(
                    out=acc[:],
                    lhsT=lhs(a).bitcast(FP8X4),
                    lhsT_scale=lhs_scale(a),
                    rhs=rq[a][:].bitcast(FP8X4),
                    rhs_scale=rqs[a][:],
                    start=(a == 0),
                    stop=(a == NPASS - 1),
                )
            return acc

        def with_v2(m, rq, rqs, n):
            cols = slice(m * P, (m + 1) * P)
            return product(lambda a: v2w[a][:, cols], lambda a: v2s[4 * a :, cols], rq, rqs, n)

        def with_w2(m, n):
            c, u = divmod(m, 2)
            cols = lambda a: slice(a * W2C + u * P, a * W2C + (u + 1) * P)
            return product(lambda a: w2q[c][:, cols(a)], lambda a: w2qs[c][:, cols(a)], hq, hqs, n)

        b_sb = {}

        def make_b(m):
            acc_b = with_v2(m, xq, xqs, m % 4)
            b_sb[m] = held([P, S], F32, "b_sb%d" % m)
            nc.scalar.copy(out=b_sb[m][:], in_=acc_b[:])

        for m in range(2):
            make_b(m)
        cast_w2(0)
        for c in range(S2 // W2C):
            pair = (2 * c, 2 * c + 1)
            acc_f, acc_e, top, diff = {}, {}, {}, {}
            for m in pair:
                acc_f[m] = with_w2(m, 4 + m % 2)
            for m in pair:
                acc_e[m] = with_v2(m, hq, hqs, 6 + m % 2)
            if c + 1 < S2 // W2C:
                cast_w2(c + 1)
                for m in pair:
                    make_b(m + 2)
            for m in pair:
                top[m] = ring.tile([P, S], F32, name="top")
                nc.vector.tensor_tensor(out=top[m][:], in0=acc_f[m][:], in1=b_sb[m][:], op=ALU.max)
            for m in pair:
                diff[m] = ring.tile([P, S], F32, name="diff", bufs=4)
                nc.vector.tensor_tensor(out=diff[m][:], in0=acc_e[m][:], in1=top[m][:], op=ALU.subtract)
            for m in pair:
                res = ring.tile([P, S], F32, name="res", bufs=4)
                eng = nc.vector if c == S2 // W2C - 1 else nc.gpsimd
                eng.tensor_tensor(out=res[:], in0=diff[m][:], in1=seat_t[m // 4][:, m % 4, :], op=ALU.mult)
                nc.sync.dma_start(out=out[m * P : (m + 1) * P, :], in_=res[:])
